import numpy as np
import ml_dtypes


def mxq(x, axis, fmt="e4m3"):
    dtype, down = {"e4m3": (ml_dtypes.float8_e4m3fn, 7), "e5m2": (ml_dtypes.float8_e5m2, 14)}[fmt]
    v = np.moveaxis(np.asarray(x, np.float32).astype(ml_dtypes.bfloat16).astype(np.float64), axis, -1)
    blocks = v.reshape(v.shape[:-1] + (-1, 32))
    amax = np.abs(blocks).max(-1, keepdims=True)
    byte = np.maximum(np.where(amax > 0, np.frexp(amax)[1] - 1 + 127, 0) - down, 1)
    scale = np.exp2(byte - 127.0)
    codes = (blocks / scale).astype(np.float32).astype(dtype).astype(np.float64)
    return np.moveaxis((codes * scale).reshape(v.shape), -1, axis)


WIDE = False


def mx_kscale(k):
    if not WIDE:
        return np.ones(k)
    levels = np.array([10, -10, 5, -5, 0])
    if k % 512:
        return np.exp2(np.random.permutation(np.resize(levels, k // 32))).repeat(32)
    a = np.empty((k // 512, 16))
    for p in range(k // 512):
        a[p, :8] = np.random.permutation(np.resize(levels, 8))
        for g in range(8):
            far = levels[np.abs(levels - a[p, g]) >= 10]
            a[p, g + 8] = far[np.random.randint(len(far))]
    return np.exp2(a.ravel()).repeat(32)


BF16 = ml_dtypes.bfloat16


def bf(x):
    return np.asarray(x, np.float32).astype(BF16)


def f64(x):
    return np.asarray(x).astype(np.float64)


E2M1 = np.array([0.0, 0.5, 1.0, 1.5, 2.0, 3.0, 4.0, 6.0, -0.0, -0.5, -1.0, -1.5, -2.0, -3.0, -4.0, -6.0])


def pack_weight(w, fmt):
    k, n = w.shape
    w = f64(bf(w)).reshape(k // 32, 32, n)
    amax = np.abs(w).max(1)
    if fmt == "e4m3":
        byte = np.frexp(amax)[1] - 1 + 127 - 7
    else:
        mant, ex = np.frexp(amax / 6.0)
        byte = np.where(mant > 0.5, ex, ex - 1) + 127
    byte = np.clip(np.where(amax > 0, byte, 1), 1, 254)
    scaled = (w * np.exp2(127.0 - byte)[:, None, :]).reshape(k, n).astype(np.float32)
    by_word = np.ascontiguousarray(scaled.reshape(k // 512, 128, 4, n).transpose(0, 1, 3, 2))
    if fmt == "e4m3":
        words = by_word.astype(ml_dtypes.float8_e4m3fn).view(np.uint8)
    else:
        c = by_word.astype(ml_dtypes.float4_e2m1fn).view(np.uint8) & 0xF
        words = c[..., 0::2] | (c[..., 1::2] << 4)
    return np.ascontiguousarray(words), np.ascontiguousarray(byte.astype(np.uint8).reshape(k // 512, 16, n))


def unpack_weight(words, scales, fmt):
    g, p, n, _ = words.shape
    if fmt == "e4m3":
        vals = np.ascontiguousarray(words).view(ml_dtypes.float8_e4m3fn).astype(np.float64)
    else:
        nib = np.empty((g, p, n, 4), np.uint8)
        nib[..., 0::2] = words & 0xF
        nib[..., 1::2] = words >> 4
        vals = E2M1[nib]
    vals = vals * np.repeat(np.exp2(scales.astype(np.float64) - 127.0), 8, axis=1)[..., None]
    return vals.transpose(0, 1, 3, 2).reshape(g * 512, n)
def pack4(w):
    words, scales = pack_weight(w, "e2m1")
    return words.reshape(words.shape[0], 128, -1), scales


def unpack4(words, scales):
    return unpack_weight(words.reshape(words.shape[0], 128, -1, 2), scales, "e2m1")


def planes(Y):
    n, m = Y.shape
    b = f64(bf(Y)).reshape(n // 32, 32, m)
    amax = np.abs(b).max(1)
    byte = np.clip(np.where(amax > 0, np.frexp(amax)[1] - 1 + 127 - 7, 1), 1, 254)
    codes = (b * np.exp2(127.0 - byte)[:, None, :]).reshape(n, m).astype(np.float32).astype(ml_dtypes.float8_e4m3fn).view(np.uint8)
    words = codes.reshape(n // 512, 128, 4, m).transpose(0, 1, 3, 2)
    return np.ascontiguousarray(words), np.ascontiguousarray(byte.astype(np.uint8).reshape(n // 512, 16, m))


M, P, K, F = 3072, 32, 1024, 1024


def setup_inputs():
    s = mx_kscale(K)
    x_words, x_scales = pack_weight(np.random.randn(K, M) * s[:, None], "e4m3")
    a = np.arange(P)
    c = np.cos(np.pi * (2 * a[:, None] + 1) * a[None, :] / (2 * P)) * np.sqrt(np.where(a == 0, 1.0, 2.0) / P)
    basis = np.kron(c, c) + 0.1 * np.random.randn(K, F) / np.sqrt(K)
    ramp = ((a[:, None] + a[None, :]) / (P - 1) - 1.0).reshape(F)
    return {
        "x_words": x_words,
        "x_scales": x_scales,
        "basis": bf(basis / s[:, None]),
        "inv_step": bf(np.exp(0.8 * np.random.randn(F))),
        "freq_pos": bf(ramp + 0.5 * np.random.randn(F)),
        "bandwidth": bf(0.5 + np.random.randn(M)),
    }


def reference(x_words, x_scales, basis, inv_step, freq_pos, bandwidth):
    x = unpack_weight(x_words, x_scales, "e4m3")
    d = mxq(f64(basis), 0, "e4m3")
    coef = x.T @ d
    keep = 1.0 / (1.0 + np.exp(f64(freq_pos)[None, :] - f64(bandwidth)[:, None]))
    y = coef * f64(inv_step)[None, :] * keep
    Y = y.T
    words, scales = planes(Y)
    return y, words, scales

@@ -1,0 +1,280 @@
+from contextlib import ExitStack
+
+import concourse.mybir as mybir
+from concourse.masks import make_identity
+
+M, K, F = 3072, 1024, 1024
+FLOPS = 2 * M * K * F
+
+F32 = mybir.dt.float32
+BF16 = mybir.dt.bfloat16
+U32 = mybir.dt.uint32
+I32 = mybir.dt.int32
+U8 = mybir.dt.uint8
+FP8X4 = mybir.dt.float8_e4m3fn_x4
+ALU = mybir.AluOpType
+ACT = mybir.ActivationFunctionType
+
+P = 128
+PACK = 4
+GROUP = P * PACK
+K_PASSES = K // GROUP
+F_GROUPS = F // GROUP
+CHUNK = 512
+CHUNKS = M // CHUNK
+M_TILES = CHUNK // P
+UNITS = F_GROUPS * CHUNKS
+EARLY = 2 * CHUNK
+LEAD = 3
+
+
+def tile_masked_cosine_patch_coefficients_g6_kernel(
+    tc, x_words, x_scales, basis, inv_step, freq_pos, bandwidth, out_0, out_1, out_2
+):
+    nc = tc.nc
+
+    with ExitStack() as ctx:
+        keepers = ctx.enter_context(tc.tile_pool(name="keepers", bufs=1))
+        stream = ctx.enter_context(tc.tile_pool(name="stream", bufs=3))
+        psum = ctx.enter_context(tc.psum_pool(name="psum", bufs=1))
+        ctx.enter_context(tc.manual_schedule())
+
+        x_rows = x_words.rearrange("g p m t -> p g (m t)")
+        words_rows = out_1.rearrange("g p m t -> p g (m t)")
+
+        xs_early = keepers.tile([P, EARLY], U8, name="xs_early", align_bytes=64)
+        xs_late = keepers.tile([P, M - EARLY], U8, name="xs_late", align_bytes=64)
+        nc.vector.memset(xs_early[:].bitcast(U32), 0)
+        nc.vector.memset(xs_late[:].bitcast(U32), 0)
+
+        pos_raw = keepers.tile([P, F_GROUPS, 16], BF16, name="pos_raw")
+        nc.scalar.dma_start(
+            out=pos_raw[:, :, 0:PACK], in_=freq_pos.rearrange("(g p t) -> p g t", p=P, t=PACK)
+        )
+        inv = keepers.tile([P, F_GROUPS, 16], BF16, name="inv")
+        nc.gpsimd.dma_start(
+            out=inv[:, :, 0:PACK], in_=inv_step.rearrange("(g p t) -> p g t", p=P, t=PACK)
+        )
+        ident = keepers.tile([P, P], F32, name="ident")
+        make_identity(nc, ident[:])
+
+        bw_first = keepers.tile([P, CHUNK], BF16, name="bw_first")
+        bw_rest = keepers.tile([P, M - CHUNK], BF16, name="bw_rest")
+        d_raw = {}
+        x_codes = []
+
+        def load_basis(g):
+            for kp in range(K_PASSES):
+                raw = keepers.tile([P, PACK, GROUP], BF16, name="d_raw_%d_%d" % (g, kp))
+                nc.sync.dma_start(
+                    out=raw[:],
+                    in_=basis[kp * GROUP : (kp + 1) * GROUP, g * GROUP : (g + 1) * GROUP].rearrange(
+                        "(p j) f -> p j f", j=PACK
+                    ),
+                )
+                d_raw[g, kp] = raw
+
+        def load_patches(c):
+            codes = keepers.tile([P, K_PASSES, CHUNK], U32, name="x_codes_%d" % c, align_bytes=64)
+            nc.sync.dma_start(
+                out=codes[:].bitcast(I32),
+                in_=x_rows[:, :, c * CHUNK * PACK : (c + 1) * CHUNK * PACK].bitcast(I32),
+            )
+            x_codes.append(codes)
+
+        def load_scales(plane, m0, m1):
+            for q in range(4):
+                nc.sync.dma_start(
+                    out=plane[32 * q : 32 * q + 4 * K_PASSES, :].bitcast(I32),
+                    in_=x_scales[:, 4 * q : 4 * q + 4, m0:m1].bitcast(I32),
+                )
+
+        nc.sync.dma_start(out=bw_first[:], in_=bandwidth[0:CHUNK].partition_broadcast(P))
+        load_basis(0)
+        load_scales(xs_early, 0, EARLY)
+        load_patches(0)
+        nc.sync.dma_start(out=bw_rest[:], in_=bandwidth[CHUNK:M].partition_broadcast(P))
+        load_patches(1)
+        load_basis(1)
+        load_scales(xs_late, EARLY, M)
+        for c in range(2, CHUNKS):
+            load_patches(c)
+
+        neg_pos = keepers.tile([P, F_GROUPS, PACK], F32, name="neg_pos")
+        nc.vector.tensor_scalar(
+            out=neg_pos[:], in0=pos_raw[:, :, 0:PACK], scalar1=-1.0, scalar2=None, op0=ALU.mult
+        )
+
+        d_grouped = {}
+        d_codes = {}
+        d_scales = {}
+
+        def group_basis(copy, g, t, kp):
+            if kp == 0:
+                d_grouped[g, t] = keepers.tile(
+                    [P, K_PASSES, P, PACK], BF16, name="d_grouped_%d_%d" % (g, t), align_bytes=64
+                )
+            copy(
+                out=d_grouped[g, t][:, kp, :, :],
+                in_=d_raw[g, kp][:].rearrange("p j (c t) -> p t c j", t=PACK)[:, t, :, :],
+            )
+
+        def quantize_basis(g, t):
+            codes = keepers.tile([P, K_PASSES * P], U32, name="d_codes_%d_%d" % (g, t), align_bytes=64)
+            scales = keepers.tile([P, K_PASSES * P], U8, name="d_scales_%d_%d" % (g, t), align_bytes=64)
+            nc.vector.quantize_mx(
+                out=codes[:].bitcast(FP8X4),
+                scales=scales[:],
+                in_=d_grouped[g, t][:].rearrange("p k c j -> p (k c j)"),
+            )
+            d_codes[g, t] = codes
+            d_scales[g, t] = scales
+
+        keep = {}
+        acc = {}
+        y_t = {}
+        y_bf = {}
+        turned = {}
+        y_rows = {}
+        y_scales = [
+            keepers.tile([P, M], U8, name="y_scales_%d" % g, align_bytes=64) for g in range(F_GROUPS)
+        ]
+
+        def mask(u):
+            g, c = divmod(u, CHUNKS)
+            src = bw_first[:] if c == 0 else bw_rest[:, (c - 1) * CHUNK : c * CHUNK]
+            keep[u] = stream.tile([P, PACK, CHUNK], F32, name="keep", bufs=LEAD + 1)
+            for t in range(PACK):
+                nc.scalar.activation(
+                    out=keep[u][:, t, :], in_=src, func=ACT.Sigmoid, bias=neg_pos[:, g, t : t + 1]
+                )
+
+        def multiply(u, t):
+            g, c = divmod(u, CHUNKS)
+            m0 = c * CHUNK
+            bank = psum.tile([P, CHUNK], F32, name="acc_%d" % t)
+            for kp in range(K_PASSES):
+                if m0 < EARLY:
+                    plane = xs_early[4 * kp : P, m0 : m0 + CHUNK]
+                else:
+                    plane = xs_late[4 * kp : P, m0 - EARLY : m0 - EARLY + CHUNK]
+                nc.tensor.matmul_mx(
+                    out=bank[:],
+                    lhsT=d_codes[g, t][:, kp * P : (kp + 1) * P].bitcast(FP8X4),
+                    lhsT_scale=d_scales[g, t][:, kp * P : (kp + 1) * P],
+                    rhs=x_codes[c][:, kp, :].bitcast(FP8X4),
+                    rhs_scale=plane,
+                    start=(kp == 0),
+                    stop=(kp == K_PASSES - 1),
+                )
+            acc[u, t] = bank
+
+        def scale_and_mask(u, t):
+            g = u // CHUNKS
+            if t == 0:
+                y_t[u] = stream.tile([P, PACK, CHUNK], F32, name="y_t")
+            nc.vector.scalar_tensor_tensor(
+                out=y_t[u][:, t, :],
+                in0=acc[u, t][:],
+                scalar=inv[:, g, t : t + 1],
+                in1=keep[u][:, t, :],
+                op0=ALU.mult,
+                op1=ALU.mult,
+            )
+
+        def turn(u):
+            for i in range(M_TILES):
+                bank = psum.tile([P, PACK, P], F32, name="turned_%d" % i)
+                for t in range(PACK):
+                    nc.tensor.transpose(bank[:, t, :], y_t[u][:, t, i * P : (i + 1) * P], ident[:])
+                turned[u, i] = bank
+
+        def copy_out(copy, u, i):
+            if i == 0:
+                y_rows[u] = stream.tile([P, M_TILES, P, PACK], F32, name="y_rows")
+            copy(out=y_rows[u][:, i, :, :], in_=turned[u, i][:].rearrange("m t p -> m p t"))
+
+        def store_rows(u, i0, i1):
+            g, c = divmod(u, CHUNKS)
+            rows = out_0[c * CHUNK : (c + 1) * CHUNK, g * GROUP : (g + 1) * GROUP]
+            nc.sync.dma_start(
+                out=rows.rearrange("(i m) f -> m i f", m=P)[:, i0:i1, :],
+                in_=y_rows[u][:, i0:i1, :, :].rearrange("m i p t -> m i (p t)"),
+            )
+
+        def round_to_bf16(u, on_gpsimd):
+            y_bf[u] = stream.tile([P, CHUNK, PACK], BF16, name="y_bf", bufs=1, align_bytes=64)
+            src = y_t[u][:].rearrange("p t m -> p m t")
+            if on_gpsimd:
+                nc.gpsimd.tensor_scalar(
+                    out=y_bf[u][:], in0=src, scalar1=1.0, scalar2=1.0, op0=ALU.mult, op1=ALU.mult
+                )
+            else:
+                nc.vector.tensor_copy(out=y_bf[u][:], in_=src)
+
+        def quantize_result(u):
+            g, c = divmod(u, CHUNKS)
+            codes = stream.tile([P, CHUNK], U32, name="y_codes", align_bytes=64)
+            nc.vector.quantize_mx(
+                out=codes[:].bitcast(FP8X4),
+                scales=y_scales[g][:, c * CHUNK : (c + 1) * CHUNK],
+                in_=y_bf[u][:].rearrange("p m t -> p (m t)"),
+            )
+            nc.sync.dma_start(
+                out=words_rows[:, g, c * CHUNK * PACK : (c + 1) * CHUNK * PACK].bitcast(I32),
+                in_=codes[:].bitcast(I32),
+            )
+
+        def store_scales(g, m0, m1):
+            for q in range(4):
+                nc.sync.dma_start(
+                    out=out_2[g, 4 * q : 4 * q + 4, m0:m1].bitcast(I32),
+                    in_=y_scales[g][32 * q : 32 * q + 4, m0:m1].bitcast(I32),
+                )
+
+        for u in range(LEAD):
+            mask(u)
+        for t in range(PACK):
+            group_basis(nc.vector.tensor_copy, 0, t, 0)
+        for t in range(PACK + 1):
+            if t < PACK:
+                group_basis(nc.vector.tensor_copy, 0, t, 1)
+            if t >= 1:
+                quantize_basis(0, t - 1)
+                multiply(0, t - 1)
+
+        last = UNITS - 1
+        for u in range(UNITS):
+            if u >= 1:
+                for t in range(PACK):
+                    multiply(u, t)
+            for t in range(PACK):
+                scale_and_mask(u, t)
+            if u < PACK:
+                for kp in range(K_PASSES):
+                    group_basis(nc.scalar.copy, 1, u, kp)
+            if 1 <= u <= PACK:
+                quantize_basis(1, u - 1)
+            if u >= 1:
+                turn(u - 1)
+                quantize_result(u - 1)
+            round_to_bf16(u, u < last)
+            if u >= 1:
+                on_vector = 2 if u <= PACK else 1
+                for i in range(M_TILES):
+                    copy_out(nc.vector.tensor_copy if i >= M_TILES - on_vector else nc.scalar.copy, u - 1, i)
+                    if i % 2 == 1:
+                        store_rows(u - 1, i - 1, i + 1)
+            if u == CHUNKS:
+                store_scales(0, 0, M)
+            if u == last:
+                store_scales(1, 0, M - CHUNK)
+            if u + LEAD < UNITS:
+                mask(u + LEAD)
+
+        turn(last)
+        quantize_result(last)
+        store_scales(1, M - CHUNK, M)
+        for i in range(M_TILES):
+            copy_out(nc.vector.tensor_copy if i == M_TILES - 1 else nc.scalar.copy, last, i)
+            store_rows(last, i, i + 1)

@@ -52,14 +52,10 @@ def tile_masked_cosine_patch_coefficients_g6_kernel(
             out=pos_raw[:, :, 0:PACK], in_=freq_pos.rearrange("(g p t) -> p g t", p=P, t=PACK)
         )
         inv = keepers.tile([P, F_GROUPS, 16], BF16, name="inv")
-        nc.gpsimd.dma_start(
-            out=inv[:, :, 0:PACK], in_=inv_step.rearrange("(g p t) -> p g t", p=P, t=PACK)
-        )
         ident = keepers.tile([P, P], F32, name="ident")
         make_identity(nc, ident[:])
 
-        bw_first = keepers.tile([P, CHUNK], BF16, name="bw_first")
-        bw_rest = keepers.tile([P, M - CHUNK], BF16, name="bw_rest")
+        cutoff = {}
         d_raw = {}
         x_codes = []
 
@@ -82,6 +78,12 @@ def tile_masked_cosine_patch_coefficients_g6_kernel(
             )
             x_codes.append(codes)
 
+        def load_cutoffs(c0, c1):
+            spread = keepers.tile([P, (c1 - c0) * CHUNK], BF16, name="cutoff_%d" % c0)
+            nc.sync.dma_start(out=spread[:], in_=bandwidth[c0 * CHUNK : c1 * CHUNK].partition_broadcast(P))
+            for c in range(c0, c1):
+                cutoff[c] = spread[:, (c - c0) * CHUNK : (c - c0 + 1) * CHUNK]
+
         def load_scales(plane, m0, m1):
             for q in range(4):
                 nc.sync.dma_start(
@@ -89,13 +91,18 @@ def tile_masked_cosine_patch_coefficients_g6_kernel(
                     in_=x_scales[:, 4 * q : 4 * q + 4, m0:m1].bitcast(I32),
                 )
 
-        nc.sync.dma_start(out=bw_first[:], in_=bandwidth[0:CHUNK].partition_broadcast(P))
+        load_cutoffs(0, 1)
         load_basis(0)
+        load_cutoffs(1, 2)
         load_scales(xs_early, 0, EARLY)
         load_patches(0)
-        nc.sync.dma_start(out=bw_rest[:], in_=bandwidth[CHUNK:M].partition_broadcast(P))
-        load_patches(1)
+        nc.sync.dma_start(
+            out=inv[:, :, 0:PACK], in_=inv_step.rearrange("(g p t) -> p g t", p=P, t=PACK)
+        )
+        load_cutoffs(2, 3)
         load_basis(1)
+        load_patches(1)
+        load_cutoffs(3, CHUNKS)
         load_scales(xs_late, EARLY, M)
         for c in range(2, CHUNKS):
             load_patches(c)
@@ -142,11 +149,10 @@ def tile_masked_cosine_patch_coefficients_g6_kernel(
 
         def mask(u):
             g, c = divmod(u, CHUNKS)
-            src = bw_first[:] if c == 0 else bw_rest[:, (c - 1) * CHUNK : c * CHUNK]
             keep[u] = stream.tile([P, PACK, CHUNK], F32, name="keep", bufs=LEAD + 1)
             for t in range(PACK):
                 nc.scalar.activation(
-                    out=keep[u][:, t, :], in_=src, func=ACT.Sigmoid, bias=neg_pos[:, g, t : t + 1]
+                    out=keep[u][:, t, :], in_=cutoff[c], func=ACT.Sigmoid, bias=neg_pos[:, g, t : t + 1]
                 )
 
         def multiply(u, t):
@@ -202,15 +208,12 @@ def tile_masked_cosine_patch_coefficients_g6_kernel(
                 in_=y_rows[u][:, i0:i1, :, :].rearrange("m i p t -> m i (p t)"),
             )
 
-        def round_to_bf16(u, on_gpsimd):
-            y_bf[u] = stream.tile([P, CHUNK, PACK], BF16, name="y_bf", bufs=1, align_bytes=64)
-            src = y_t[u][:].rearrange("p t m -> p m t")
-            if on_gpsimd:
-                nc.gpsimd.tensor_scalar(
-                    out=y_bf[u][:], in0=src, scalar1=1.0, scalar2=1.0, op0=ALU.mult, op1=ALU.mult
-                )
-            else:
-                nc.vector.tensor_copy(out=y_bf[u][:], in_=src)
+        def round_to_bf16(u):
+            y_bf[u] = stream.tile([P, CHUNK, PACK], BF16, name="y_bf", bufs=2, align_bytes=64)
+            nc.vector.tensor_copy(
+                out=y_bf[u][:].rearrange("p (c i) t -> p c t i", i=2),
+                in_=y_t[u][:].rearrange("p t (c i) -> p c t i", i=2),
+            )
 
         def quantize_result(u):
             g, c = divmod(u, CHUNKS)
@@ -252,17 +255,16 @@ def tile_masked_cosine_patch_coefficients_g6_kernel(
                 scale_and_mask(u, t)
             if u < PACK:
                 for kp in range(K_PASSES):
-                    group_basis(nc.scalar.copy, 1, u, kp)
+                    group_basis(nc.scalar.copy if u < 2 else nc.vector.tensor_copy, 1, u, kp)
             if 1 <= u <= PACK:
                 quantize_basis(1, u - 1)
             if u >= 1:
                 turn(u - 1)
                 quantize_result(u - 1)
-            round_to_bf16(u, u < last)
+            round_to_bf16(u)
             if u >= 1:
-                on_vector = 2 if u <= PACK else 1
                 for i in range(M_TILES):
-                    copy_out(nc.vector.tensor_copy if i >= M_TILES - on_vector else nc.scalar.copy, u - 1, i)
+                    copy_out(nc.scalar.copy, u - 1, i)
                     if i % 2 == 1:
                         store_rows(u - 1, i - 1, i + 1)
             if u == CHUNKS:
@@ -276,5 +278,5 @@ def tile_masked_cosine_patch_coefficients_g6_kernel(
         quantize_result(last)
         store_scales(1, M - CHUNK, M)
         for i in range(M_TILES):
-            copy_out(nc.vector.tensor_copy if i == M_TILES - 1 else nc.scalar.copy, last, i)
+            copy_out(nc.scalar.copy, last, i)
             store_rows(last, i, i + 1)

@@ -26,6 +26,7 @@ M_TILES = CHUNK // P
 UNITS = F_GROUPS * CHUNKS
 EARLY = 2 * CHUNK
 LEAD = 3
+PAIRS = CHUNKS // 2
 
 
 def tile_masked_cosine_patch_coefficients_g6_kernel(
@@ -47,8 +48,12 @@ def tile_masked_cosine_patch_coefficients_g6_kernel(
         nc.vector.memset(xs_early[:].bitcast(U32), 0)
         nc.vector.memset(xs_late[:].bitcast(U32), 0)
 
+        bw_raw = keepers.tile([P, PAIRS, 16], BF16, name="bw_raw")
+        nc.sync.dma_start(
+            out=bw_raw[:, :, 0 : 2 * PACK], in_=bandwidth.rearrange("(h p j) -> p h j", p=P, j=2 * PACK)
+        )
         pos_raw = keepers.tile([P, F_GROUPS, 16], BF16, name="pos_raw")
-        nc.scalar.dma_start(
+        nc.sync.dma_start(
             out=pos_raw[:, :, 0:PACK], in_=freq_pos.rearrange("(g p t) -> p g t", p=P, t=PACK)
         )
         inv = keepers.tile([P, F_GROUPS, 16], BF16, name="inv")
@@ -57,7 +62,7 @@ def tile_masked_cosine_patch_coefficients_g6_kernel(
 
         cutoff = {}
         d_raw = {}
-        x_codes = []
+        x_codes = {}
 
         def load_basis(g):
             for kp in range(K_PASSES):
@@ -70,19 +75,15 @@ def tile_masked_cosine_patch_coefficients_g6_kernel(
                 )
                 d_raw[g, kp] = raw
 
-        def load_patches(c):
-            codes = keepers.tile([P, K_PASSES, CHUNK], U32, name="x_codes_%d" % c, align_bytes=64)
+        def load_patches(c0, c1):
+            width = (c1 - c0) * CHUNK
+            codes = keepers.tile([P, K_PASSES, width], U32, name="x_codes_%d" % c0, align_bytes=64)
             nc.sync.dma_start(
                 out=codes[:].bitcast(I32),
-                in_=x_rows[:, :, c * CHUNK * PACK : (c + 1) * CHUNK * PACK].bitcast(I32),
+                in_=x_rows[:, :, c0 * CHUNK * PACK : c1 * CHUNK * PACK].bitcast(I32),
             )
-            x_codes.append(codes)
-
-        def load_cutoffs(c0, c1):
-            spread = keepers.tile([P, (c1 - c0) * CHUNK], BF16, name="cutoff_%d" % c0)
-            nc.sync.dma_start(out=spread[:], in_=bandwidth[c0 * CHUNK : c1 * CHUNK].partition_broadcast(P))
             for c in range(c0, c1):
-                cutoff[c] = spread[:, (c - c0) * CHUNK : (c - c0 + 1) * CHUNK]
+                x_codes[c] = codes[:, :, (c - c0) * CHUNK : (c - c0 + 1) * CHUNK]
 
         def load_scales(plane, m0, m1):
             for q in range(4):
@@ -91,21 +92,17 @@ def tile_masked_cosine_patch_coefficients_g6_kernel(
                     in_=x_scales[:, 4 * q : 4 * q + 4, m0:m1].bitcast(I32),
                 )
 
-        load_cutoffs(0, 1)
         load_basis(0)
-        load_cutoffs(1, 2)
         load_scales(xs_early, 0, EARLY)
-        load_patches(0)
+        load_patches(0, 1)
         nc.sync.dma_start(
             out=inv[:, :, 0:PACK], in_=inv_step.rearrange("(g p t) -> p g t", p=P, t=PACK)
         )
-        load_cutoffs(2, 3)
-        load_basis(1)
-        load_patches(1)
-        load_cutoffs(3, CHUNKS)
+        load_patches(1, 2)
         load_scales(xs_late, EARLY, M)
-        for c in range(2, CHUNKS):
-            load_patches(c)
+        load_basis(1)
+        for c in range(2, CHUNKS, 2):
+            load_patches(c, c + 2)
 
         neg_pos = keepers.tile([P, F_GROUPS, PACK], F32, name="neg_pos")
         nc.vector.tensor_scalar(
@@ -235,7 +232,26 @@ def tile_masked_cosine_patch_coefficients_g6_kernel(
                     in_=y_scales[g][32 * q : 32 * q + 4, m0:m1].bitcast(I32),
                 )
 
-        for u in range(LEAD):
+        bw_words = bw_raw[:].bitcast(F32)
+        spread_banks = []
+        for h in range(PAIRS):
+            bank = psum.tile([P, PACK, P], F32, name="turned_%d" % h)
+            for w in range(PACK):
+                nc.tensor.transpose(bank[:, w, :], bw_words[:, h, w : w + 1].to_broadcast([P, P]), ident[:])
+            spread_banks.append(bank)
+
+        def spread_cutoffs(h):
+            spread = keepers.tile([P, P, PACK], F32, name="cutoff_%d" % h)
+            nc.scalar.copy(out=spread[:], in_=spread_banks[h][:].rearrange("q w p -> q p w"))
+            values = spread[:].rearrange("q p w -> q (p w)").bitcast(BF16)
+            for half in range(2):
+                cutoff[2 * h + half] = values[:, half * CHUNK : (half + 1) * CHUNK]
+
+        spread_cutoffs(0)
+        mask(0)
+        for h in range(1, PAIRS):
+            spread_cutoffs(h)
+        for u in range(1, LEAD):
             mask(u)
         for t in range(PACK):
             group_basis(nc.vector.tensor_copy, 0, t, 0)
@@ -253,11 +269,11 @@ def tile_masked_cosine_patch_coefficients_g6_kernel(
                     multiply(u, t)
             for t in range(PACK):
                 scale_and_mask(u, t)
-            if u < PACK:
-                for kp in range(K_PASSES):
-                    group_basis(nc.scalar.copy if u < 2 else nc.vector.tensor_copy, 1, u, kp)
             if 1 <= u <= PACK:
-                quantize_basis(1, u - 1)
+                for kp in range(K_PASSES):
+                    group_basis(nc.vector.tensor_copy, 1, u - 1, kp)
+            if 2 <= u <= PACK + 1:
+                quantize_basis(1, u - 2)
             if u >= 1:
                 turn(u - 1)
                 quantize_result(u - 1)

@@ -24,8 +24,9 @@ CHUNK = 512
 CHUNKS = M // CHUNK
 M_TILES = CHUNK // P
 UNITS = F_GROUPS * CHUNKS
-EARLY = 2 * CHUNK
-LEAD = 3
+EARLY = CHUNK
+LEAD = 2
+ON_GPSIMD = 384
 PAIRS = CHUNKS // 2
 
 
@@ -98,9 +99,9 @@ def tile_masked_cosine_patch_coefficients_g6_kernel(
         nc.sync.dma_start(
             out=inv[:, :, 0:PACK], in_=inv_step.rearrange("(g p t) -> p g t", p=P, t=PACK)
         )
-        load_patches(1, 2)
-        load_scales(xs_late, EARLY, M)
         load_basis(1)
+        load_scales(xs_late, EARLY, M)
+        load_patches(1, 2)
         for c in range(2, CHUNKS, 2):
             load_patches(c, c + 2)
 
@@ -114,7 +115,9 @@ def tile_masked_cosine_patch_coefficients_g6_kernel(
         d_scales = {}
 
         def group_basis(copy, g, t, kp):
-            if kp == 0:
+            if kp == 0 and (g, t) == (F_GROUPS - 1, PACK - 1):
+                d_grouped[g, t] = stream.tile([P, K_PASSES, P, PACK], BF16, name="y_bf", bufs=1, align_bytes=64)
+            elif kp == 0:
                 d_grouped[g, t] = keepers.tile(
                     [P, K_PASSES, P, PACK], BF16, name="d_grouped_%d_%d" % (g, t), align_bytes=64
                 )
@@ -140,12 +143,10 @@ def tile_masked_cosine_patch_coefficients_g6_kernel(
         y_bf = {}
         turned = {}
         y_rows = {}
-        y_scales = [
-            keepers.tile([P, M], U8, name="y_scales_%d" % g, align_bytes=64) for g in range(F_GROUPS)
-        ]
+        y_scales = keepers.tile([P, M], U8, name="y_scales", align_bytes=64)
 
         def mask(u):
-            g, c = divmod(u, CHUNKS)
+            c, g = divmod(u, F_GROUPS)
             keep[u] = stream.tile([P, PACK, CHUNK], F32, name="keep", bufs=LEAD + 1)
             for t in range(PACK):
                 nc.scalar.activation(
@@ -153,7 +154,7 @@ def tile_masked_cosine_patch_coefficients_g6_kernel(
                 )
 
         def multiply(u, t):
-            g, c = divmod(u, CHUNKS)
+            c, g = divmod(u, F_GROUPS)
             m0 = c * CHUNK
             bank = psum.tile([P, CHUNK], F32, name="acc_%d" % t)
             for kp in range(K_PASSES):
@@ -173,7 +174,7 @@ def tile_masked_cosine_patch_coefficients_g6_kernel(
             acc[u, t] = bank
 
         def scale_and_mask(u, t):
-            g = u // CHUNKS
+            g = u % F_GROUPS
             if t == 0:
                 y_t[u] = stream.tile([P, PACK, CHUNK], F32, name="y_t")
             nc.vector.scalar_tensor_tensor(
@@ -193,31 +194,42 @@ def tile_masked_cosine_patch_coefficients_g6_kernel(
                 turned[u, i] = bank
 
         def copy_out(copy, u, i):
-            if i == 0:
-                y_rows[u] = stream.tile([P, M_TILES, P, PACK], F32, name="y_rows")
-            copy(out=y_rows[u][:, i, :, :], in_=turned[u, i][:].rearrange("m t p -> m p t"))
+            c, g = divmod(u, F_GROUPS)
+            if g == 0 and i == 0:
+                y_rows[c] = stream.tile([P, M_TILES, F_GROUPS, P, PACK], F32, name="y_rows")
+            copy(out=y_rows[c][:, i, g, :, :], in_=turned[u, i][:].rearrange("m t p -> m p t"))
 
-        def store_rows(u, i0, i1):
-            g, c = divmod(u, CHUNKS)
-            rows = out_0[c * CHUNK : (c + 1) * CHUNK, g * GROUP : (g + 1) * GROUP]
+        def store_rows(c, i, g0, g1):
+            m0 = c * CHUNK + i * P
             nc.sync.dma_start(
-                out=rows.rearrange("(i m) f -> m i f", m=P)[:, i0:i1, :],
-                in_=y_rows[u][:, i0:i1, :, :].rearrange("m i p t -> m i (p t)"),
+                out=out_0[m0 : m0 + P, g0 * GROUP : g1 * GROUP],
+                in_=y_rows[c][:, i, g0:g1, :, :].rearrange("m g p t -> m (g p t)"),
             )
 
-        def round_to_bf16(u):
-            y_bf[u] = stream.tile([P, CHUNK, PACK], BF16, name="y_bf", bufs=2, align_bytes=64)
+        def round_on_gpsimd(u):
+            y_bf[u] = stream.tile([P, CHUNK, PACK], BF16, name="y_bf", bufs=1, align_bytes=64)
+            nc.gpsimd.tensor_scalar(
+                out=y_bf[u][:, 0:ON_GPSIMD, :],
+                in0=y_t[u][:, :, 0:ON_GPSIMD].rearrange("p t m -> p m t"),
+                scalar1=1.0,
+                scalar2=1.0,
+                op0=ALU.mult,
+                op1=ALU.mult,
+            )
+
+        def round_on_vector(u, m0):
+            if m0 == 0:
+                y_bf[u] = stream.tile([P, CHUNK, PACK], BF16, name="y_bf", bufs=1, align_bytes=64)
             nc.vector.tensor_copy(
-                out=y_bf[u][:].rearrange("p (c i) t -> p c t i", i=2),
-                in_=y_t[u][:].rearrange("p t (c i) -> p c t i", i=2),
+                out=y_bf[u][:, m0:CHUNK, :], in_=y_t[u][:, :, m0:CHUNK].rearrange("p t m -> p m t")
             )
 
         def quantize_result(u):
-            g, c = divmod(u, CHUNKS)
+            c, g = divmod(u, F_GROUPS)
             codes = stream.tile([P, CHUNK], U32, name="y_codes", align_bytes=64)
             nc.vector.quantize_mx(
                 out=codes[:].bitcast(FP8X4),
-                scales=y_scales[g][:, c * CHUNK : (c + 1) * CHUNK],
+                scales=y_scales[4 * g : P, c * CHUNK : (c + 1) * CHUNK],
                 in_=y_bf[u][:].rearrange("p m t -> p (m t)"),
             )
             nc.sync.dma_start(
@@ -225,11 +237,11 @@ def tile_masked_cosine_patch_coefficients_g6_kernel(
                 in_=codes[:].bitcast(I32),
             )
 
-        def store_scales(g, m0, m1):
+        def store_scales(m0, m1):
             for q in range(4):
                 nc.sync.dma_start(
-                    out=out_2[g, 4 * q : 4 * q + 4, m0:m1].bitcast(I32),
-                    in_=y_scales[g][32 * q : 32 * q + 4, m0:m1].bitcast(I32),
+                    out=out_2[:, 4 * q : 4 * q + 4, m0:m1].bitcast(I32),
+                    in_=y_scales[32 * q : 32 * q + 4 * F_GROUPS, m0:m1].bitcast(I32),
                 )
 
         bw_words = bw_raw[:].bitcast(F32)
@@ -248,10 +260,7 @@ def tile_masked_cosine_patch_coefficients_g6_kernel(
                 cutoff[2 * h + half] = values[:, half * CHUNK : (half + 1) * CHUNK]
 
         spread_cutoffs(0)
-        mask(0)
-        for h in range(1, PAIRS):
-            spread_cutoffs(h)
-        for u in range(1, LEAD):
+        for u in range(LEAD):
             mask(u)
         for t in range(PACK):
             group_basis(nc.vector.tensor_copy, 0, t, 0)
@@ -261,38 +270,50 @@ def tile_masked_cosine_patch_coefficients_g6_kernel(
             if t >= 1:
                 quantize_basis(0, t - 1)
                 multiply(0, t - 1)
+        for t in range(PACK):
+            scale_and_mask(0, t)
+        for t in range(PACK):
+            for kp in range(K_PASSES):
+                group_basis(nc.scalar.copy if t < 2 else nc.vector.tensor_copy, 1, t, kp)
+            if t >= 2:
+                quantize_basis(1, t - 2)
+        for t in range(2, PACK):
+            quantize_basis(1, t)
+        for h in range(1, PAIRS):
+            spread_cutoffs(h)
+        mask(LEAD)
+        round_on_gpsimd(0)
 
         last = UNITS - 1
-        for u in range(UNITS):
-            if u >= 1:
-                for t in range(PACK):
-                    multiply(u, t)
+        for u in range(1, UNITS):
             for t in range(PACK):
+                multiply(u, t)
+            for t in range(PACK - 1):
                 scale_and_mask(u, t)
-            if 1 <= u <= PACK:
-                for kp in range(K_PASSES):
-                    group_basis(nc.vector.tensor_copy, 1, u - 1, kp)
-            if 2 <= u <= PACK + 1:
-                quantize_basis(1, u - 2)
-            if u >= 1:
-                turn(u - 1)
-                quantize_result(u - 1)
-            round_to_bf16(u)
-            if u >= 1:
-                for i in range(M_TILES):
-                    copy_out(nc.scalar.copy, u - 1, i)
-                    if i % 2 == 1:
-                        store_rows(u - 1, i - 1, i + 1)
-            if u == CHUNKS:
-                store_scales(0, 0, M)
-            if u == last:
-                store_scales(1, 0, M - CHUNK)
-            if u + LEAD < UNITS:
+            round_on_vector(u - 1, ON_GPSIMD)
+            scale_and_mask(u, PACK - 1)
+            turn(u - 1)
+            quantize_result(u - 1)
+            if u < last:
+                round_on_gpsimd(u)
+            else:
+                store_scales(0, M - CHUNK)
+                round_on_vector(u, 0)
+            c, g = divmod(u - 1, F_GROUPS)
+            masks_left = u + LEAD < UNITS
+            for i in range(M_TILES):
+                copy_out(nc.vector.tensor_copy if masks_left and i == M_TILES - 1 else nc.scalar.copy, u - 1, i)
+                if c >= CHUNKS - 2:
+                    store_rows(c, i, g, g + 1)
+                elif g == F_GROUPS - 1:
+                    store_rows(c, i, 0, F_GROUPS)
+            if masks_left:
                 mask(u + LEAD)
 
         turn(last)
-        quantize_result(last)
-        store_scales(1, M - CHUNK, M)
-        for i in range(M_TILES):
-            copy_out(nc.scalar.copy, last, i)
-            store_rows(last, i, i + 1)
+        for i in (0, 3, 1, 2):
+            copy_out(nc.vector.tensor_copy if i == M_TILES - 1 else nc.scalar.copy, last, i)
+            if i == 2:
+                quantize_result(last)
+            store_rows(CHUNKS - 1, i, 1, F_GROUPS)
+        store_scales(M - CHUNK, M)

@@ -26,7 +26,8 @@ M_TILES = CHUNK // P
 UNITS = F_GROUPS * CHUNKS
 EARLY = CHUNK
 LEAD = 2
-ON_GPSIMD = 384
+HALF = CHUNK // 2
+PAIRS_OF_FOUR = ((0, 1), (2, 3))
 PAIRS = CHUNKS // 2
 
 
@@ -116,7 +117,7 @@ def tile_masked_cosine_patch_coefficients_g6_kernel(
 
         def group_basis(copy, g, t, kp):
             if kp == 0 and (g, t) == (F_GROUPS - 1, PACK - 1):
-                d_grouped[g, t] = stream.tile([P, K_PASSES, P, PACK], BF16, name="y_bf", bufs=1, align_bytes=64)
+                d_grouped[g, t] = stream.tile([P, K_PASSES, P, PACK], BF16, name="y_bf_gpsimd", bufs=1, align_bytes=64)
             elif kp == 0:
                 d_grouped[g, t] = keepers.tile(
                     [P, K_PASSES, P, PACK], BF16, name="d_grouped_%d_%d" % (g, t), align_bytes=64
@@ -141,14 +142,16 @@ def tile_masked_cosine_patch_coefficients_g6_kernel(
         acc = {}
         y_t = {}
         y_bf = {}
+        y_codes = {}
         turned = {}
         y_rows = {}
         y_scales = keepers.tile([P, M], U8, name="y_scales", align_bytes=64)
 
-        def mask(u):
+        def mask(u, slots):
             c, g = divmod(u, F_GROUPS)
-            keep[u] = stream.tile([P, PACK, CHUNK], F32, name="keep", bufs=LEAD + 1)
-            for t in range(PACK):
+            if u not in keep:
+                keep[u] = stream.tile([P, PACK, CHUNK], F32, name="keep", bufs=LEAD + 1)
+            for t in slots:
                 nc.scalar.activation(
                     out=keep[u][:, t, :], in_=cutoff[c], func=ACT.Sigmoid, bias=neg_pos[:, g, t : t + 1]
                 )
@@ -186,8 +189,8 @@ def tile_masked_cosine_patch_coefficients_g6_kernel(
                 op1=ALU.mult,
             )
 
-        def turn(u):
-            for i in range(M_TILES):
+        def turn(u, tiles):
+            for i in tiles:
                 bank = psum.tile([P, PACK, P], F32, name="turned_%d" % i)
                 for t in range(PACK):
                     nc.tensor.transpose(bank[:, t, :], y_t[u][:, t, i * P : (i + 1) * P], ident[:])
@@ -206,35 +209,40 @@ def tile_masked_cosine_patch_coefficients_g6_kernel(
                 in_=y_rows[c][:, i, g0:g1, :, :].rearrange("m g p t -> m (g p t)"),
             )
 
-        def round_on_gpsimd(u):
-            y_bf[u] = stream.tile([P, CHUNK, PACK], BF16, name="y_bf", bufs=1, align_bytes=64)
+        def round_on_gpsimd(u, half):
+            y_bf[u, half] = stream.tile([P, HALF, PACK], BF16, name="y_bf_gpsimd", bufs=1, align_bytes=64)
             nc.gpsimd.tensor_scalar(
-                out=y_bf[u][:, 0:ON_GPSIMD, :],
-                in0=y_t[u][:, :, 0:ON_GPSIMD].rearrange("p t m -> p m t"),
+                out=y_bf[u, half][:],
+                in0=y_t[u][:, :, half * HALF : (half + 1) * HALF].rearrange("p t m -> p m t"),
                 scalar1=1.0,
                 scalar2=1.0,
                 op0=ALU.mult,
                 op1=ALU.mult,
             )
 
-        def round_on_vector(u, m0):
-            if m0 == 0:
-                y_bf[u] = stream.tile([P, CHUNK, PACK], BF16, name="y_bf", bufs=1, align_bytes=64)
+        def round_on_vector(u, half):
+            y_bf[u, half] = stream.tile([P, HALF, PACK], BF16, name="y_bf_vector", bufs=2, align_bytes=64)
             nc.vector.tensor_copy(
-                out=y_bf[u][:, m0:CHUNK, :], in_=y_t[u][:, :, m0:CHUNK].rearrange("p t m -> p m t")
+                out=y_bf[u, half][:],
+                in_=y_t[u][:, :, half * HALF : (half + 1) * HALF].rearrange("p t m -> p m t"),
             )
 
-        def quantize_result(u):
+        def quantize_result(u, half):
             c, g = divmod(u, F_GROUPS)
-            codes = stream.tile([P, CHUNK], U32, name="y_codes", align_bytes=64)
+            if u not in y_codes:
+                y_codes[u] = stream.tile([P, CHUNK], U32, name="y_codes", align_bytes=64)
+            m0 = c * CHUNK + half * HALF
             nc.vector.quantize_mx(
-                out=codes[:].bitcast(FP8X4),
-                scales=y_scales[4 * g : P, c * CHUNK : (c + 1) * CHUNK],
-                in_=y_bf[u][:].rearrange("p m t -> p (m t)"),
+                out=y_codes[u][:, half * HALF : (half + 1) * HALF].bitcast(FP8X4),
+                scales=y_scales[4 * g : P, m0 : m0 + HALF],
+                in_=y_bf[u, half][:].rearrange("p m t -> p (m t)"),
             )
+
+        def store_words(u):
+            c, g = divmod(u, F_GROUPS)
             nc.sync.dma_start(
                 out=words_rows[:, g, c * CHUNK * PACK : (c + 1) * CHUNK * PACK].bitcast(I32),
-                in_=codes[:].bitcast(I32),
+                in_=y_codes[u][:].bitcast(I32),
             )
 
         def store_scales(m0, m1):
@@ -261,7 +269,7 @@ def tile_masked_cosine_patch_coefficients_g6_kernel(
 
         spread_cutoffs(0)
         for u in range(LEAD):
-            mask(u)
+            mask(u, range(PACK))
         for t in range(PACK):
             group_basis(nc.vector.tensor_copy, 0, t, 0)
         for t in range(PACK + 1):
@@ -277,43 +285,47 @@ def tile_masked_cosine_patch_coefficients_g6_kernel(
                 group_basis(nc.scalar.copy if t < 2 else nc.vector.tensor_copy, 1, t, kp)
             if t >= 2:
                 quantize_basis(1, t - 2)
-        for t in range(2, PACK):
-            quantize_basis(1, t)
+        quantize_basis(1, 2)
+        round_on_vector(0, 1)
+        quantize_basis(1, 3)
+        round_on_gpsimd(0, 0)
         for h in range(1, PAIRS):
             spread_cutoffs(h)
-        mask(LEAD)
-        round_on_gpsimd(0)
+        mask(LEAD, range(PACK))
 
         last = UNITS - 1
         for u in range(1, UNITS):
-            for t in range(PACK):
-                multiply(u, t)
-            for t in range(PACK - 1):
-                scale_and_mask(u, t)
-            round_on_vector(u - 1, ON_GPSIMD)
-            scale_and_mask(u, PACK - 1)
-            turn(u - 1)
-            quantize_result(u - 1)
+            c, g = divmod(u - 1, F_GROUPS)
+            masks_left = u + LEAD < UNITS
+            for pair in PAIRS_OF_FOUR:
+                for t in pair:
+                    multiply(u, t)
+                    scale_and_mask(u, t)
+                turn(u - 1, pair)
+                for i in pair:
+                    copy_out(nc.vector.tensor_copy if masks_left and i == 0 else nc.scalar.copy, u - 1, i)
+                    if c == 0 or c >= CHUNKS - 2:
+                        store_rows(c, i, g, g + 1)
+                    elif g == F_GROUPS - 1:
+                        store_rows(c, i, 0, F_GROUPS)
+                if masks_left:
+                    mask(u + LEAD, pair)
+            quantize_result(u - 1, 1)
+            round_on_vector(u, 1)
+            quantize_result(u - 1, 0)
+            store_words(u - 1)
             if u < last:
-                round_on_gpsimd(u)
+                round_on_gpsimd(u, 0)
             else:
                 store_scales(0, M - CHUNK)
                 round_on_vector(u, 0)
-            c, g = divmod(u - 1, F_GROUPS)
-            masks_left = u + LEAD < UNITS
-            for i in range(M_TILES):
-                copy_out(nc.vector.tensor_copy if masks_left and i == M_TILES - 1 else nc.scalar.copy, u - 1, i)
-                if c >= CHUNKS - 2:
-                    store_rows(c, i, g, g + 1)
-                elif g == F_GROUPS - 1:
-                    store_rows(c, i, 0, F_GROUPS)
-            if masks_left:
-                mask(u + LEAD)
 
-        turn(last)
+        turn(last, range(M_TILES))
+        quantize_result(last, 1)
         for i in (0, 3, 1, 2):
             copy_out(nc.vector.tensor_copy if i == M_TILES - 1 else nc.scalar.copy, last, i)
             if i == 2:
-                quantize_result(last)
+                quantize_result(last, 0)
+                store_words(last)
             store_rows(CHUNKS - 1, i, 1, F_GROUPS)
         store_scales(M - CHUNK, M)

from contextlib import ExitStack

import concourse.mybir as mybir
from concourse.masks import make_identity

M, K, F = 3072, 1024, 1024
FLOPS = 2 * M * K * F

F32 = mybir.dt.float32
BF16 = mybir.dt.bfloat16
U32 = mybir.dt.uint32
I32 = mybir.dt.int32
U8 = mybir.dt.uint8
FP8X4 = mybir.dt.float8_e4m3fn_x4
ALU = mybir.AluOpType
ACT = mybir.ActivationFunctionType

P = 128
PACK = 4
GROUP = P * PACK
K_PASSES = K // GROUP
F_GROUPS = F // GROUP
CHUNK = 512
CHUNKS = M // CHUNK
M_TILES = CHUNK // P
UNITS = F_GROUPS * CHUNKS
EARLY = CHUNK
LEAD = 2
HALF = CHUNK // 2
PAIRS_OF_FOUR = ((0, 1), (2, 3))
PAIRS = CHUNKS // 2


def tile_masked_cosine_patch_coefficients_g6_kernel(
    tc, x_words, x_scales, basis, inv_step, freq_pos, bandwidth, out_0, out_1, out_2
):
    nc = tc.nc

    with ExitStack() as ctx:
        keepers = ctx.enter_context(tc.tile_pool(name="keepers", bufs=1))
        stream = ctx.enter_context(tc.tile_pool(name="stream", bufs=3))
        psum = ctx.enter_context(tc.psum_pool(name="psum", bufs=1))
        ctx.enter_context(tc.manual_schedule())

        x_rows = x_words.rearrange("g p m t -> p g (m t)")
        words_rows = out_1.rearrange("g p m t -> p g (m t)")

        xs_early = keepers.tile([P, EARLY], U8, name="xs_early", align_bytes=64)
        xs_late = keepers.tile([P, M - EARLY], U8, name="xs_late", align_bytes=64)
        nc.vector.memset(xs_early[:].bitcast(U32), 0)
        nc.vector.memset(xs_late[:].bitcast(U32), 0)

        bw_raw = keepers.tile([P, PAIRS, 16], BF16, name="bw_raw")
        nc.sync.dma_start(
            out=bw_raw[:, :, 0 : 2 * PACK], in_=bandwidth.rearrange("(h p j) -> p h j", p=P, j=2 * PACK)
        )
        pos_raw = keepers.tile([P, F_GROUPS, 16], BF16, name="pos_raw")
        nc.sync.dma_start(
            out=pos_raw[:, :, 0:PACK], in_=freq_pos.rearrange("(g p t) -> p g t", p=P, t=PACK)
        )
        inv = keepers.tile([P, F_GROUPS, 16], BF16, name="inv")
        ident = keepers.tile([P, P], F32, name="ident")
        make_identity(nc, ident[:])

        cutoff = {}
        d_raw = {}
        x_codes = {}

        def load_basis(g):
            for kp in range(K_PASSES):
                raw = keepers.tile([P, PACK, GROUP], BF16, name="d_raw_%d_%d" % (g, kp))
                nc.sync.dma_start(
                    out=raw[:],
                    in_=basis[kp * GROUP : (kp + 1) * GROUP, g * GROUP : (g + 1) * GROUP].rearrange(
                        "(p j) f -> p j f", j=PACK
                    ),
                )
                d_raw[g, kp] = raw

        def load_patches(c0, c1):
            width = (c1 - c0) * CHUNK
            codes = keepers.tile([P, K_PASSES, width], U32, name="x_codes_%d" % c0, align_bytes=64)
            nc.sync.dma_start(
                out=codes[:].bitcast(I32),
                in_=x_rows[:, :, c0 * CHUNK * PACK : c1 * CHUNK * PACK].bitcast(I32),
            )
            for c in range(c0, c1):
                x_codes[c] = codes[:, :, (c - c0) * CHUNK : (c - c0 + 1) * CHUNK]

        def load_scales(plane, m0, m1):
            for q in range(4):
                nc.sync.dma_start(
                    out=plane[32 * q : 32 * q + 4 * K_PASSES, :].bitcast(I32),
                    in_=x_scales[:, 4 * q : 4 * q + 4, m0:m1].bitcast(I32),
                )

        load_basis(0)
        load_scales(xs_early, 0, EARLY)
        load_patches(0, 1)
        nc.sync.dma_start(
            out=inv[:, :, 0:PACK], in_=inv_step.rearrange("(g p t) -> p g t", p=P, t=PACK)
        )
        load_basis(1)
        load_scales(xs_late, EARLY, M)
        load_patches(1, 2)
        for c in range(2, CHUNKS, 2):
            load_patches(c, c + 2)

        neg_pos = keepers.tile([P, F_GROUPS, PACK], F32, name="neg_pos")
        nc.vector.tensor_scalar(
            out=neg_pos[:], in0=pos_raw[:, :, 0:PACK], scalar1=-1.0, scalar2=None, op0=ALU.mult
        )

        d_grouped = {}
        d_codes = {}
        d_scales = {}

        def group_basis(copy, g, t, kp):
            if kp == 0 and (g, t) == (F_GROUPS - 1, PACK - 1):
                d_grouped[g, t] = stream.tile([P, K_PASSES, P, PACK], BF16, name="y_bf_gpsimd", bufs=1, align_bytes=64)
            elif kp == 0:
                d_grouped[g, t] = keepers.tile(
                    [P, K_PASSES, P, PACK], BF16, name="d_grouped_%d_%d" % (g, t), align_bytes=64
                )
            copy(
                out=d_grouped[g, t][:, kp, :, :],
                in_=d_raw[g, kp][:].rearrange("p j (c t) -> p t c j", t=PACK)[:, t, :, :],
            )

        def quantize_basis(g, t):
            codes = keepers.tile([P, K_PASSES * P], U32, name="d_codes_%d_%d" % (g, t), align_bytes=64)
            scales = keepers.tile([P, K_PASSES * P], U8, name="d_scales_%d_%d" % (g, t), align_bytes=64)
            nc.vector.quantize_mx(
                out=codes[:].bitcast(FP8X4),
                scales=scales[:],
                in_=d_grouped[g, t][:].rearrange("p k c j -> p (k c j)"),
            )
            d_codes[g, t] = codes
            d_scales[g, t] = scales

        keep = {}
        acc = {}
        y_t = {}
        y_bf = {}
        y_codes = {}
        turned = {}
        y_rows = {}
        y_scales = keepers.tile([P, M], U8, name="y_scales", align_bytes=64)

        def mask(u, slots):
            c, g = divmod(u, F_GROUPS)
            if u not in keep:
                keep[u] = stream.tile([P, PACK, CHUNK], F32, name="keep", bufs=LEAD + 1)
            for t in slots:
                nc.scalar.activation(
                    out=keep[u][:, t, :], in_=cutoff[c], func=ACT.Sigmoid, bias=neg_pos[:, g, t : t + 1]
                )

        def multiply(u, t):
            c, g = divmod(u, F_GROUPS)
            m0 = c * CHUNK
            bank = psum.tile([P, CHUNK], F32, name="acc_%d" % t)
            for kp in range(K_PASSES):
                if m0 < EARLY:
                    plane = xs_early[4 * kp : P, m0 : m0 + CHUNK]
                else:
                    plane = xs_late[4 * kp : P, m0 - EARLY : m0 - EARLY + CHUNK]
                nc.tensor.matmul_mx(
                    out=bank[:],
                    lhsT=d_codes[g, t][:, kp * P : (kp + 1) * P].bitcast(FP8X4),
                    lhsT_scale=d_scales[g, t][:, kp * P : (kp + 1) * P],
                    rhs=x_codes[c][:, kp, :].bitcast(FP8X4),
                    rhs_scale=plane,
                    start=(kp == 0),
                    stop=(kp == K_PASSES - 1),
                )
            acc[u, t] = bank

        def scale_and_mask(u, t):
            g = u % F_GROUPS
            if t == 0:
                y_t[u] = stream.tile([P, PACK, CHUNK], F32, name="y_t")
            nc.vector.scalar_tensor_tensor(
                out=y_t[u][:, t, :],
                in0=acc[u, t][:],
                scalar=inv[:, g, t : t + 1],
                in1=keep[u][:, t, :],
                op0=ALU.mult,
                op1=ALU.mult,
            )

        def turn(u, tiles):
            for i in tiles:
                bank = psum.tile([P, PACK, P], F32, name="turned_%d" % i)
                for t in range(PACK):
                    nc.tensor.transpose(bank[:, t, :], y_t[u][:, t, i * P : (i + 1) * P], ident[:])
                turned[u, i] = bank

        def copy_out(copy, u, i):
            c, g = divmod(u, F_GROUPS)
            if g == 0 and i == 0:
                y_rows[c] = stream.tile([P, M_TILES, F_GROUPS, P, PACK], F32, name="y_rows")
            copy(out=y_rows[c][:, i, g, :, :], in_=turned[u, i][:].rearrange("m t p -> m p t"))

        def store_rows(c, i, g0, g1):
            m0 = c * CHUNK + i * P
            nc.sync.dma_start(
                out=out_0[m0 : m0 + P, g0 * GROUP : g1 * GROUP],
                in_=y_rows[c][:, i, g0:g1, :, :].rearrange("m g p t -> m (g p t)"),
            )

        def round_on_gpsimd(u, half):
            y_bf[u, half] = stream.tile([P, HALF, PACK], BF16, name="y_bf_gpsimd", bufs=1, align_bytes=64)
            nc.gpsimd.tensor_scalar(
                out=y_bf[u, half][:],
                in0=y_t[u][:, :, half * HALF : (half + 1) * HALF].rearrange("p t m -> p m t"),
                scalar1=1.0,
                scalar2=1.0,
                op0=ALU.mult,
                op1=ALU.mult,
            )

        def round_on_vector(u, half):
            y_bf[u, half] = stream.tile([P, HALF, PACK], BF16, name="y_bf_vector", bufs=2, align_bytes=64)
            nc.vector.tensor_copy(
                out=y_bf[u, half][:],
                in_=y_t[u][:, :, half * HALF : (half + 1) * HALF].rearrange("p t m -> p m t"),
            )

        def quantize_result(u, half):
            c, g = divmod(u, F_GROUPS)
            if u not in y_codes:
                y_codes[u] = stream.tile([P, CHUNK], U32, name="y_codes", align_bytes=64)
            m0 = c * CHUNK + half * HALF
            nc.vector.quantize_mx(
                out=y_codes[u][:, half * HALF : (half + 1) * HALF].bitcast(FP8X4),
                scales=y_scales[4 * g : P, m0 : m0 + HALF],
                in_=y_bf[u, half][:].rearrange("p m t -> p (m t)"),
            )

        def store_words(u):
            c, g = divmod(u, F_GROUPS)
            nc.sync.dma_start(
                out=words_rows[:, g, c * CHUNK * PACK : (c + 1) * CHUNK * PACK].bitcast(I32),
                in_=y_codes[u][:].bitcast(I32),
            )

        def store_scales(m0, m1):
            for q in range(4):
                nc.sync.dma_start(
                    out=out_2[:, 4 * q : 4 * q + 4, m0:m1].bitcast(I32),
                    in_=y_scales[32 * q : 32 * q + 4 * F_GROUPS, m0:m1].bitcast(I32),
                )

        bw_words = bw_raw[:].bitcast(F32)
        spread_banks = []
        for h in range(PAIRS):
            bank = psum.tile([P, PACK, P], F32, name="turned_%d" % h)
            for w in range(PACK):
                nc.tensor.transpose(bank[:, w, :], bw_words[:, h, w : w + 1].to_broadcast([P, P]), ident[:])
            spread_banks.append(bank)

        def spread_cutoffs(h):
            spread = keepers.tile([P, P, PACK], F32, name="cutoff_%d" % h)
            nc.scalar.copy(out=spread[:], in_=spread_banks[h][:].rearrange("q w p -> q p w"))
            values = spread[:].rearrange("q p w -> q (p w)").bitcast(BF16)
            for half in range(2):
                cutoff[2 * h + half] = values[:, half * CHUNK : (half + 1) * CHUNK]

        spread_cutoffs(0)
        for u in range(LEAD):
            mask(u, range(PACK))
        for t in range(PACK):
            group_basis(nc.vector.tensor_copy, 0, t, 0)
        for t in range(PACK + 1):
            if t < PACK:
                group_basis(nc.vector.tensor_copy, 0, t, 1)
            if t >= 1:
                quantize_basis(0, t - 1)
                multiply(0, t - 1)
        for t in range(PACK):
            scale_and_mask(0, t)
        for t in range(PACK):
            for kp in range(K_PASSES):
                group_basis(nc.scalar.copy if t < 2 else nc.vector.tensor_copy, 1, t, kp)
            if t >= 2:
                quantize_basis(1, t - 2)
        quantize_basis(1, 2)
        round_on_vector(0, 1)
        quantize_basis(1, 3)
        round_on_gpsimd(0, 0)
        for h in range(1, PAIRS):
            spread_cutoffs(h)
        mask(LEAD, range(PACK))

        last = UNITS - 1
        for u in range(1, UNITS):
            c, g = divmod(u - 1, F_GROUPS)
            masks_left = u + LEAD < UNITS
            for pair in PAIRS_OF_FOUR:
                for t in pair:
                    multiply(u, t)
                    scale_and_mask(u, t)
                turn(u - 1, pair)
                for i in pair:
                    copy_out(nc.vector.tensor_copy if masks_left and i == 0 else nc.scalar.copy, u - 1, i)
                    if c == 0 or c >= CHUNKS - 2:
                        store_rows(c, i, g, g + 1)
                    elif g == F_GROUPS - 1:
                        store_rows(c, i, 0, F_GROUPS)
                if masks_left:
                    mask(u + LEAD, pair)
            quantize_result(u - 1, 1)
            round_on_vector(u, 1)
            quantize_result(u - 1, 0)
            store_words(u - 1)
            if u < last:
                round_on_gpsimd(u, 0)
            else:
                store_scales(0, M - CHUNK)
                round_on_vector(u, 0)

        turn(last, range(M_TILES))
        quantize_result(last, 1)
        for i in (0, 3, 1, 2):
            copy_out(nc.vector.tensor_copy if i == M_TILES - 1 else nc.scalar.copy, last, i)
            if i == 2:
                quantize_result(last, 0)
                store_words(last)
            store_rows(CHUNKS - 1, i, 1, F_GROUPS)
        store_scales(M - CHUNK, M)
